import numpy as np, ml_dtypes
CORES = [113,118,241,246]
N = 4
NH, QP = 4, 128
def setup_inputs(rng):
    return {"q": rng.standard_normal((N, 128, NH * QP), dtype=np.float32).astype(ml_dtypes.bfloat16), "k": rng.standard_normal((N, 128, NH * 128), dtype=np.float32).astype(ml_dtypes.bfloat16), "v": rng.standard_normal((N, 128, NH * 128), dtype=np.float32).astype(ml_dtypes.bfloat16)}
def setup_inputs_big(rng):
    d = setup_inputs(rng)
    for k in ("q", "k", "v"): d[k] = (d[k].astype(np.float32) * 1024.0).astype(d[k].dtype)
    return d
def setup_inputs_small(rng):
    d = setup_inputs(rng)
    for k in ("q", "k", "v"): d[k] = (d[k].astype(np.float32) * (1 / 1024.0)).astype(d[k].dtype)
    return d
def setup_inputs_apart(rng):
    d = setup_inputs(rng)
    f = (10.0 ** rng.permutation(np.linspace(-1.5, 1.5, N))).astype(np.float32).reshape(N, 1, 1)
    for k in ("q", "k", "v"): d[k] = (d[k].astype(np.float32) * f).astype(d[k].dtype)
    return d
def reference(q, k, v):
    Q, K, V = q.astype(np.float64), k.astype(np.float64), v.astype(np.float64)
    y = np.zeros((N, 128, NH * QP))
    for r in range(N):
        for h in range(NH):
            for j in range(N):
                S = np.maximum(K[j][:, 128 * h:128 * h + 128].T @ Q[r][:, QP * h:QP * h + QP], 0.0)
                y[r][:, QP * h:QP * h + QP] += V[j][:, 128 * h:128 * h + 128].T @ S
    return {"y": y.astype(ml_dtypes.bfloat16 if q.dtype != np.float64 else np.float64)}

@@ -1,0 +1,227 @@
+from concourse.bass import DstId, RemoteDMATransfer
+from concourse.mybir import dt, AluOpType
+
+NHH = 2
+P = 128
+WH = P * NHH
+WD = 4 * P - WH
+NU = 12
+
+SCRATCH = {
+    "kv": ("sbuf", [P, 1024], "bfloat16"),
+    "qo": ("sbuf", [P, 512], "bfloat16"),
+    "kvp": ("sbuf", [P, 1024], "bfloat16"),
+    "kvt": ("sbuf", [P, 1024], "bfloat16"),
+    "kvc": ("sbuf", [P, max(2 * WD, 8)], "bfloat16"),
+    "qp": ("sbuf", [P, max(WH, 8)], "bfloat16"),
+    "sb": ("sbuf", [P, 2048], "bfloat16"),
+    "zero": ("sbuf", [P, 256], "float32"),
+    "ops": ("sbuf", [P, max(WH, 8)], "bfloat16"),
+    "opr": ("sbuf", [P, max(WH, 8)], "bfloat16"),
+    "yo": ("sbuf", [P, 512], "bfloat16"),
+    "ps": ("psum", [P, 4096], "float32"),
+}
+SEMAPHORES = (["lkH", "lvH", "lqH", "lkD", "lvD", "lqD", "z", "sent", "atH", "aq", "apH", "apD", "atD", "ac", "ao",
+               "fD", "fH", "stD", "stH"] + ["ao%d" % h for h in range(4)]
+              + [n + str(i) for i in range(NU) for n in ("s", "r", "po", "pc")])
+
+
+def rank_program(g, core, T, topo):
+    if T.rank_of(core) is None:
+        return
+    S = T.sem
+
+    def same_chip(a, b):
+        return topo.host(a) == topo.host(b) and topo.chip(a) == topo.chip(b)
+
+    others = [c for c in T.cores if c != core]
+    peer = [c for c in others if same_chip(c, core)][0]
+    far = [c for c in others if not same_chip(c, core)]
+    twin = [c for c in far if topo.die(c) == topo.die(core)][0]
+    cross = [c for c in far if c != twin][0]
+    off = topo.mask(core, twin)
+    on = topo.mask(core, peer)
+    hi = on & ~off
+
+    def n1(m):
+        return bin(m).count("1")
+
+    Hh, Dh = list(range(NHH)), list(range(NHH, 4))
+    HK = 2 * WH
+
+    g.vector.memset(T.zero[:], 0.0).then_inc(S.z, 1)
+    g.vector.wait_ge(S.z, 1)
+    if Hh:
+        g.sync.dma_start(T.kv[:, 0:WH], T.k[:, 0:WH]).then_inc(S.lkH, 16)
+        g.scalar.dma_start(T.kv[:, WH:HK], T.v[:, 0:WH]).then_inc(S.lvH, 16)
+        g.sync.dma_start(T.qo[:, 0:WH], T.q[:, 0:WH]).then_inc(S.lqH, 16)
+    if Dh:
+        g.scalar.dma_start(T.kv[:, HK:HK + WD], T.k[:, WH:512]).then_inc(S.lkD, 16)
+        g.sync.dma_start(T.kv[:, HK + WD:1024], T.v[:, WH:512]).then_inc(S.lvD, 16)
+        g.scalar.dma_start(T.qo[:, WH:512], T.q[:, WH:512]).then_inc(S.lqD, 16)
+
+    sent = [0]
+
+    def send(trs):
+        if len(trs) == 1:
+            src, d, dst, sem, m = trs[0]
+            rid, pid = topo.addr(d, core)
+            g.remote_dma(out_ap=dst, in_ap=src, remote_sem=sem, local_sem=S.sent, pid=pid, routing_id=rid,
+                         dma_engine_mask=m)
+        else:
+            lst = []
+            for src, d, dst, sem, m in trs:
+                rid, pid = topo.addr(d, core)
+                lst.append(RemoteDMATransfer(dst_ids=[DstId(rid=rid, pnc=pid)], dma_engine_mask=m, remote_sem=sem,
+                                             src=src, dst=dst))
+            g.remote_dma_fused(lst, local_sem=S.sent)
+        sent[0] += sum(n1(t[4]) for t in trs)
+
+    mpH = hi if Dh else on
+    tH_twin = (T.kv[:, 0:HK], twin, T.kvt[:, 0:HK], S.atH, off)
+    tH_peer = (T.kv[:, 0:HK], peer, T.kvp[:, 0:HK], S.apH, mpH)
+    tq_peer = (T.qo[:, 0:WH], peer, T.qp[:, 0:WH], S.aq, hi)
+    tD_twin = (T.kv[:, HK:1024], twin, T.kvt[:, HK:1024], S.atD, off)
+    tD_cross = (T.kv[:, HK:1024], cross, T.kvc[:, 0:2 * WD], S.ac, off)
+    tD_peer = (T.kv[:, HK:1024], peer, T.kvp[:, HK:1024], S.apD, hi)
+    if Hh:
+        g.wait_ge(S.lkH, 16)
+        g.wait_ge(S.lvH, 16)
+        send([tH_twin])
+        g.wait_ge(S.lqH, 16)
+        send([tq_peer])
+    if Dh:
+        g.wait_ge(S.lkD, 16)
+        g.wait_ge(S.lvD, 16)
+        if Hh and WH == WD:
+            send([tD_twin, tH_peer])
+            send([tD_cross, tD_peer])
+        elif Hh:
+            send([tD_twin])
+            send([tH_peer])
+            send([tD_cross, tD_peer])
+        else:
+            send([tD_twin, tD_peer])
+            send([tD_cross])
+    else:
+        send([tH_peer])
+
+    units = []
+
+    def stage(waits, own, heads, buf, base, gran, drain=False):
+        for i in range(0, len(heads), gran):
+            units.append({"w": waits if i == 0 else [], "own": own, "h": heads[i:i + gran], "buf": buf, "base": base,
+                          "drain": drain and i == 0})
+
+    if Hh:
+        stage([("lkH", 16), ("lvH", 16), ("lqH", 16)], True, Hh, T.kv, 0, 2)
+    if Dh:
+        stage([("lkD", 16), ("lvD", 16), ("lqD", 16)], True, Dh, T.kv, 0, 2)
+    if Hh:
+        stage([("atH", n1(off)), ("aq", n1(hi))], False, Hh, T.kvt, 0, 1)
+        stage([], True, Hh, T.kvt, 0, 2, drain=True)
+        stage([("apH", n1(mpH))], True, Hh, T.kvp, 0, 2)
+    if Dh:
+        if not Hh:
+            stage([("apD", n1(hi))], True, Dh, T.kvp, 0, 2)
+        stage([("atD", n1(off))], True, Dh, T.kvt, 0, 2)
+        if Hh:
+            stage([("apD", n1(hi))], True, Dh, T.kvp, 0, 2)
+        stage([("ac", n1(off))], True, Dh, T.kvc, HK, 1)
+    tot = [sum(1 for u in units if u["own"] and h in u["h"]) for h in range(4)]
+    done = [0, 0, 0, 0]
+    col = 0
+    for u in units:
+        u["sb"] = col
+        col += P * len(u["h"])
+
+    def kc(h):
+        return h * P if h < NHH else HK + (h - NHH) * P
+
+    def vc(h):
+        return WH + h * P if h < NHH else HK + WD + (h - NHH) * P
+
+    waited = set()
+
+    def twait(name, val):
+        if (name, val) not in waited:
+            waited.add((name, val))
+            g.tensor.wait_ge(S[name], val)
+
+    pool = {"n": 0, "rel": [None] * 4}
+
+    def bank(release):
+        b = pool["n"] % 4
+        pool["n"] += 1
+        if pool["rel"][b]:
+            twait(pool["rel"][b], 1)
+        pool["rel"][b] = release
+        return b * 512
+
+    def emit_s(i, u):
+        for name, val in u["w"]:
+            twait(name, val)
+        c0 = bank("r%d" % i)
+        n = P * len(u["h"])
+        q = T.qo if u["own"] else T.qp
+        for m, h in enumerate(u["h"]):
+            kk = kc(h) - u["base"]
+            g.tensor.matmul(T.ps[:, c0 + m * P:c0 + (m + 1) * P], u["buf"][:, kk:kk + P], q[:, h * P:(h + 1) * P],
+                            True, True).then_inc(S["s%d" % i], 1)
+        g.vector.wait_ge(S["s%d" % i], len(u["h"]))
+        g.vector.tensor_tensor(T.sb[:, u["sb"]:u["sb"] + n], T.ps[:, c0:c0 + n], T.zero[:, 0:n],
+                               AluOpType.max).then_inc(S["r%d" % i], 1)
+
+    def emit_o(i, u):
+        twait("r%d" % i, 1)
+        n = P * len(u["h"])
+        if u["own"]:
+            for m, h in enumerate(u["h"]):
+                vv = vc(h) - u["base"]
+                a0 = 2048 + h * 512
+                g.tensor.matmul(T.ps[:, a0:a0 + P], u["buf"][:, vv:vv + P], T.sb[:, u["sb"] + m * P:u["sb"] + (m + 1) * P],
+                                done[h] == 0, done[h] == tot[h] - 1).then_inc(S["ao%d" % h], 1)
+                done[h] += 1
+                if done[h] == tot[h] and h >= NHH:
+                    g.vector.wait_ge(S["ao%d" % h], tot[h])
+                    g.vector.tensor_copy(T.yo[:, h * P:(h + 1) * P], T.ps[:, a0:a0 + P]).then_inc(S.fD, 1)
+        else:
+            c1 = bank("pc%d" % i)
+            for m, h in enumerate(u["h"]):
+                vv = vc(h) - u["base"]
+                g.tensor.matmul(T.ps[:, c1 + m * P:c1 + (m + 1) * P], u["buf"][:, vv:vv + P],
+                                T.sb[:, u["sb"] + m * P:u["sb"] + (m + 1) * P], True, True).then_inc(S["po%d" % i], 1)
+            h0 = u["h"][0]
+            g.vector.wait_ge(S["po%d" % i], len(u["h"]))
+            g.vector.tensor_copy(T.ops[:, h0 * P:h0 * P + n], T.ps[:, c1:c1 + n]).then_inc(S["pc%d" % i], 1)
+
+    pend = None
+    for i, u in enumerate(units):
+        if pend is not None and (u["w"] or u["drain"]):
+            emit_o(pend, units[pend])
+            pend = None
+        emit_s(i, u)
+        if pend is not None:
+            emit_o(pend, units[pend])
+        pend = i
+    emit_o(pend, units[pend])
+
+    if Hh:
+        for i, u in enumerate(units):
+            if not u["own"]:
+                g.wait_ge(S["pc%d" % i], 1)
+        send([(T.ops[:, 0:WH], peer, T.opr[:, 0:WH], S.ao, on)])
+        g.vector.wait_ge(S.ao, n1(on))
+        for h in Hh:
+            a0 = 2048 + h * 512
+            g.vector.wait_ge(S["ao%d" % h], tot[h])
+            g.vector.tensor_tensor(T.yo[:, h * P:(h + 1) * P], T.ps[:, a0:a0 + P], T.opr[:, h * P:(h + 1) * P],
+                                   AluOpType.add).then_inc(S.fH, 1)
+        g.scalar.wait_ge(S.fH, len(Hh))
+        g.scalar.dma_start(T.y[:, 0:WH], T.yo[:, 0:WH]).then_inc(S.stH, 16)
+        g.scalar.wait_ge(S.stH, 16)
+    if Dh:
+        g.sync.wait_ge(S.fD, len(Dh))
+        g.sync.dma_start(T.y[:, WH:512], T.yo[:, WH:512]).then_inc(S.stD, 16)
+        g.sync.wait_ge(S.stD, 16)
+    g.wait_ge(S.sent, sent[0])

@@ -1,29 +1,28 @@
 from concourse.bass import DstId, RemoteDMATransfer
-from concourse.mybir import dt, AluOpType
+from concourse.mybir import dt, AluOpType, ActivationFunctionType
 
-NHH = 2
 P = 128
-WH = P * NHH
-WD = 4 * P - WH
-NU = 12
+NT = 16
+TOT = [2, 2, 2, 3]
 
 SCRATCH = {
     "kv": ("sbuf", [P, 1024], "bfloat16"),
     "qo": ("sbuf", [P, 512], "bfloat16"),
-    "kvp": ("sbuf", [P, 1024], "bfloat16"),
     "kvt": ("sbuf", [P, 1024], "bfloat16"),
-    "kvc": ("sbuf", [P, max(2 * WD, 8)], "bfloat16"),
-    "qp": ("sbuf", [P, max(WH, 8)], "bfloat16"),
-    "sb": ("sbuf", [P, 2048], "bfloat16"),
-    "zero": ("sbuf", [P, 256], "float32"),
-    "ops": ("sbuf", [P, max(WH, 8)], "bfloat16"),
-    "opr": ("sbuf", [P, max(WH, 8)], "bfloat16"),
+    "kvc": ("sbuf", [P, 256], "bfloat16"),
+    "qp": ("sbuf", [P, 512], "bfloat16"),
+    "sb": ("sbuf", [P, NT * P], "bfloat16"),
+    "zero": ("sbuf", [P, P], "float32"),
+    "ops": ("sbuf", [P, 512], "bfloat16"),
+    "opr": ("sbuf", [P, 512], "bfloat16"),
     "yo": ("sbuf", [P, 512], "bfloat16"),
     "ps": ("psum", [P, 4096], "float32"),
 }
-SEMAPHORES = (["lkH", "lvH", "lqH", "lkD", "lvD", "lqD", "z", "sent", "atH", "aq", "apH", "apD", "atD", "ac", "ao",
-               "fD", "fH", "stD", "stH"] + ["ao%d" % h for h in range(4)]
-              + [n + str(i) for i in range(NU) for n in ("s", "r", "po", "pc")])
+SEMAPHORES = (["lk01", "lv01", "lq01", "lk2", "lv2", "lk3", "lv3", "lq23", "z", "sent",
+               "at01", "at2", "at3", "ac3", "aq01", "aq23", "ar01", "ar23",
+               "fA", "f2", "f3", "stA", "st2", "st3"]
+              + [n + str(h) for h in range(4) for n in ("ao", "po", "pc")]
+              + [n + str(i) for i in range(NT) for n in ("s", "r")])
 
 
 def rank_program(g, core, T, topo):
@@ -40,25 +39,29 @@ def rank_program(g, core, T, topo):
     twin = [c for c in far if topo.die(c) == topo.die(core)][0]
     cross = [c for c in far if c != twin][0]
     off = topo.mask(core, twin)
-    on = topo.mask(core, peer)
-    hi = on & ~off
+    hi = topo.mask(core, peer) & ~off
+    bits = [1 << b for b in range(off.bit_length()) if off >> b & 1]
+    offa, offb = sum(bits[:len(bits) // 2]), sum(bits[len(bits) // 2:])
 
     def n1(m):
         return bin(m).count("1")
 
-    Hh, Dh = list(range(NHH)), list(range(NHH, 4))
-    HK = 2 * WH
+    def kc(h):
+        return h * P if h < 2 else 512 + (h - 2) * 256
+
+    def vc(h):
+        return 256 + h * P if h < 2 else 640 + (h - 2) * 256
 
     g.vector.memset(T.zero[:], 0.0).then_inc(S.z, 1)
     g.vector.wait_ge(S.z, 1)
-    if Hh:
-        g.sync.dma_start(T.kv[:, 0:WH], T.k[:, 0:WH]).then_inc(S.lkH, 16)
-        g.scalar.dma_start(T.kv[:, WH:HK], T.v[:, 0:WH]).then_inc(S.lvH, 16)
-        g.sync.dma_start(T.qo[:, 0:WH], T.q[:, 0:WH]).then_inc(S.lqH, 16)
-    if Dh:
-        g.scalar.dma_start(T.kv[:, HK:HK + WD], T.k[:, WH:512]).then_inc(S.lkD, 16)
-        g.sync.dma_start(T.kv[:, HK + WD:1024], T.v[:, WH:512]).then_inc(S.lvD, 16)
-        g.scalar.dma_start(T.qo[:, WH:512], T.q[:, WH:512]).then_inc(S.lqD, 16)
+    g.sync.dma_start(T.kv[:, 0:256], T.k[:, 0:256]).then_inc(S.lk01, 16)
+    g.scalar.dma_start(T.kv[:, 256:512], T.v[:, 0:256]).then_inc(S.lv01, 16)
+    g.sync.dma_start(T.kv[:, kc(2):kc(2) + P], T.k[:, 256:384]).then_inc(S.lk2, 16)
+    g.scalar.dma_start(T.kv[:, vc(2):vc(2) + P], T.v[:, 256:384]).then_inc(S.lv2, 16)
+    g.sync.dma_start(T.qo[:, 0:256], T.q[:, 0:256]).then_inc(S.lq01, 16)
+    g.scalar.dma_start(T.qo[:, 256:512], T.q[:, 256:512]).then_inc(S.lq23, 16)
+    g.sync.dma_start(T.kv[:, kc(3):kc(3) + P], T.k[:, 384:512]).then_inc(S.lk3, 16)
+    g.scalar.dma_start(T.kv[:, vc(3):vc(3) + P], T.v[:, 384:512]).then_inc(S.lv3, 16)
 
     sent = [0]
 
@@ -77,151 +80,138 @@ def rank_program(g, core, T, topo):
             g.remote_dma_fused(lst, local_sem=S.sent)
         sent[0] += sum(n1(t[4]) for t in trs)
 
-    mpH = hi if Dh else on
-    tH_twin = (T.kv[:, 0:HK], twin, T.kvt[:, 0:HK], S.atH, off)
-    tH_peer = (T.kv[:, 0:HK], peer, T.kvp[:, 0:HK], S.apH, mpH)
-    tq_peer = (T.qo[:, 0:WH], peer, T.qp[:, 0:WH], S.aq, hi)
-    tD_twin = (T.kv[:, HK:1024], twin, T.kvt[:, HK:1024], S.atD, off)
-    tD_cross = (T.kv[:, HK:1024], cross, T.kvc[:, 0:2 * WD], S.ac, off)
-    tD_peer = (T.kv[:, HK:1024], peer, T.kvp[:, HK:1024], S.apD, hi)
-    if Hh:
-        g.wait_ge(S.lkH, 16)
-        g.wait_ge(S.lvH, 16)
-        send([tH_twin])
-        g.wait_ge(S.lqH, 16)
-        send([tq_peer])
-    if Dh:
-        g.wait_ge(S.lkD, 16)
-        g.wait_ge(S.lvD, 16)
-        if Hh and WH == WD:
-            send([tD_twin, tH_peer])
-            send([tD_cross, tD_peer])
-        elif Hh:
-            send([tD_twin])
-            send([tH_peer])
-            send([tD_cross, tD_peer])
-        else:
-            send([tD_twin, tD_peer])
-            send([tD_cross])
-    else:
-        send([tH_peer])
+    g.wait_ge(S.lk01, 16)
+    g.wait_ge(S.lv01, 16)
+    send([(T.kv[:, 0:512], twin, T.kvt[:, 0:512], S.at01, off)])
+    g.wait_ge(S.lk2, 16)
+    g.wait_ge(S.lv2, 16)
+    g.wait_ge(S.lq01, 16)
+    send([(T.kv[:, 512:768], twin, T.kvt[:, 512:768], S.at2, off),
+          (T.qo[:, 0:256], peer, T.qp[:, 0:256], S.aq01, hi)])
+    g.wait_ge(S.lk3, 16)
+    g.wait_ge(S.lv3, 16)
+    g.wait_ge(S.lq23, 16)
+    send([(T.kv[:, 768:1024], twin, T.kvt[:, 768:1024], S.at3, offa),
+          (T.kv[:, 768:1024], cross, T.kvc[:, 0:256], S.ac3, offb),
+          (T.qo[:, 256:512], peer, T.qp[:, 256:512], S.aq23, hi)])
 
-    units = []
-
-    def stage(waits, own, heads, buf, base, gran, drain=False):
-        for i in range(0, len(heads), gran):
-            units.append({"w": waits if i == 0 else [], "own": own, "h": heads[i:i + gran], "buf": buf, "base": base,
-                          "drain": drain and i == 0})
-
-    if Hh:
-        stage([("lkH", 16), ("lvH", 16), ("lqH", 16)], True, Hh, T.kv, 0, 2)
-    if Dh:
-        stage([("lkD", 16), ("lvD", 16), ("lqD", 16)], True, Dh, T.kv, 0, 2)
-    if Hh:
-        stage([("atH", n1(off)), ("aq", n1(hi))], False, Hh, T.kvt, 0, 1)
-        stage([], True, Hh, T.kvt, 0, 2, drain=True)
-        stage([("apH", n1(mpH))], True, Hh, T.kvp, 0, 2)
-    if Dh:
-        if not Hh:
-            stage([("apD", n1(hi))], True, Dh, T.kvp, 0, 2)
-        stage([("atD", n1(off))], True, Dh, T.kvt, 0, 2)
-        if Hh:
-            stage([("apD", n1(hi))], True, Dh, T.kvp, 0, 2)
-        stage([("ac", n1(off))], True, Dh, T.kvc, HK, 1)
-    tot = [sum(1 for u in units if u["own"] and h in u["h"]) for h in range(4)]
-    done = [0, 0, 0, 0]
-    col = 0
-    for u in units:
-        u["sb"] = col
-        col += P * len(u["h"])
-
-    def kc(h):
-        return h * P if h < NHH else HK + (h - NHH) * P
-
-    def vc(h):
-        return WH + h * P if h < NHH else HK + WD + (h - NHH) * P
-
+    nof, nhi = n1(off), n1(hi)
     waited = set()
 
-    def twait(name, val):
+    def twait(name, val=1):
         if (name, val) not in waited:
             waited.add((name, val))
             g.tensor.wait_ge(S[name], val)
 
-    pool = {"n": 0, "rel": [None] * 4}
+    tile = {}
+    done = [0] * 4
 
-    def bank(release):
-        b = pool["n"] % 4
-        pool["n"] += 1
-        if pool["rel"][b]:
-            twait(pool["rel"][b], 1)
-        pool["rel"][b] = release
-        return b * 512
-
-    def emit_s(i, u):
-        for name, val in u["w"]:
-            twait(name, val)
-        c0 = bank("r%d" % i)
-        n = P * len(u["h"])
-        q = T.qo if u["own"] else T.qp
-        for m, h in enumerate(u["h"]):
-            kk = kc(h) - u["base"]
-            g.tensor.matmul(T.ps[:, c0 + m * P:c0 + (m + 1) * P], u["buf"][:, kk:kk + P], q[:, h * P:(h + 1) * P],
-                            True, True).then_inc(S["s%d" % i], 1)
-        g.vector.wait_ge(S["s%d" % i], len(u["h"]))
-        g.vector.tensor_tensor(T.sb[:, u["sb"]:u["sb"] + n], T.ps[:, c0:c0 + n], T.zero[:, 0:n],
-                               AluOpType.max).then_inc(S["r%d" % i], 1)
-
-    def emit_o(i, u):
-        twait("r%d" % i, 1)
-        n = P * len(u["h"])
-        if u["own"]:
-            for m, h in enumerate(u["h"]):
-                vv = vc(h) - u["base"]
-                a0 = 2048 + h * 512
-                g.tensor.matmul(T.ps[:, a0:a0 + P], u["buf"][:, vv:vv + P], T.sb[:, u["sb"] + m * P:u["sb"] + (m + 1) * P],
-                                done[h] == 0, done[h] == tot[h] - 1).then_inc(S["ao%d" % h], 1)
-                done[h] += 1
-                if done[h] == tot[h] and h >= NHH:
-                    g.vector.wait_ge(S["ao%d" % h], tot[h])
-                    g.vector.tensor_copy(T.yo[:, h * P:(h + 1) * P], T.ps[:, a0:a0 + P]).then_inc(S.fD, 1)
+    def s_(key, buf, base, h, who):
+        i = len(tile)
+        tile[key] = i
+        if i >= 2:
+            twait("r%d" % (i - 2))
+        c0 = (i % 2) * 512
+        kk = kc(h) - base
+        q = T.qo if who == "own" else T.qp
+        g.tensor.matmul(T.ps[:, c0:c0 + P], buf[:, kk:kk + P], q[:, h * P:(h + 1) * P],
+                        True, True).then_inc(S["s%d" % i], 1)
+        if who == "peer":
+            g.vector.wait_ge(S["s%d" % i], 1)
+            g.vector.tensor_tensor(T.sb[:, i * P:(i + 1) * P], T.ps[:, c0:c0 + P], T.zero[:, 0:P],
+                                   AluOpType.max).then_inc(S["r%d" % i], 1)
         else:
-            c1 = bank("pc%d" % i)
-            for m, h in enumerate(u["h"]):
-                vv = vc(h) - u["base"]
-                g.tensor.matmul(T.ps[:, c1 + m * P:c1 + (m + 1) * P], u["buf"][:, vv:vv + P],
-                                T.sb[:, u["sb"] + m * P:u["sb"] + (m + 1) * P], True, True).then_inc(S["po%d" % i], 1)
-            h0 = u["h"][0]
-            g.vector.wait_ge(S["po%d" % i], len(u["h"]))
-            g.vector.tensor_copy(T.ops[:, h0 * P:h0 * P + n], T.ps[:, c1:c1 + n]).then_inc(S["pc%d" % i], 1)
+            g.scalar.wait_ge(S["s%d" % i], 1)
+            g.scalar.activation(T.sb[:, i * P:(i + 1) * P], T.ps[:, c0:c0 + P],
+                                ActivationFunctionType.Relu).then_inc(S["r%d" % i], 1)
 
-    pend = None
-    for i, u in enumerate(units):
-        if pend is not None and (u["w"] or u["drain"]):
-            emit_o(pend, units[pend])
-            pend = None
-        emit_s(i, u)
-        if pend is not None:
-            emit_o(pend, units[pend])
-        pend = i
-    emit_o(pend, units[pend])
+    def o_(key, buf, base, h):
+        i = tile[key]
+        twait("r%d" % i)
+        vv = vc(h) - base
+        a0 = (2 + h) * 512
+        g.tensor.matmul(T.ps[:, a0:a0 + P], buf[:, vv:vv + P], T.sb[:, i * P:(i + 1) * P],
+                        done[h] == 0, done[h] == TOT[h] - 1).then_inc(S["ao%d" % h], 1)
+        done[h] += 1
 
-    if Hh:
-        for i, u in enumerate(units):
-            if not u["own"]:
-                g.wait_ge(S["pc%d" % i], 1)
-        send([(T.ops[:, 0:WH], peer, T.opr[:, 0:WH], S.ao, on)])
-        g.vector.wait_ge(S.ao, n1(on))
-        for h in Hh:
-            a0 = 2048 + h * 512
-            g.vector.wait_ge(S["ao%d" % h], tot[h])
-            g.vector.tensor_tensor(T.yo[:, h * P:(h + 1) * P], T.ps[:, a0:a0 + P], T.opr[:, h * P:(h + 1) * P],
-                                   AluOpType.add).then_inc(S.fH, 1)
-        g.scalar.wait_ge(S.fH, len(Hh))
-        g.scalar.dma_start(T.y[:, 0:WH], T.yo[:, 0:WH]).then_inc(S.stH, 16)
-        g.scalar.wait_ge(S.stH, 16)
-    if Dh:
-        g.sync.wait_ge(S.fD, len(Dh))
-        g.sync.dma_start(T.y[:, WH:512], T.yo[:, WH:512]).then_inc(S.stD, 16)
-        g.sync.wait_ge(S.stD, 16)
+    def p_(h, bank, parts, free):
+        if free:
+            twait(free)
+        a0 = bank * 512
+        for n, (key, buf) in enumerate(parts):
+            i = tile[key]
+            twait("r%d" % i)
+            g.tensor.matmul(T.ps[:, a0:a0 + P], buf[:, vc(h):vc(h) + P], T.sb[:, i * P:(i + 1) * P],
+                            n == 0, n == len(parts) - 1).then_inc(S["po%d" % h], 1)
+        g.vector.wait_ge(S["po%d" % h], len(parts))
+        g.vector.tensor_copy(T.ops[:, h * P:(h + 1) * P], T.ps[:, a0:a0 + P]).then_inc(S["pc%d" % h], 1)
+
+    twait("lk01", 16)
+    twait("lq01", 16)
+    s_("o0r", T.kv, 0, 0, "own")
+    s_("o1r", T.kv, 0, 1, "own")
+    twait("lv01", 16)
+    o_("o0r", T.kv, 0, 0)
+    o_("o1r", T.kv, 0, 1)
+    twait("lk2", 16)
+    twait("lk3", 16)
+    twait("lq23", 16)
+    s_("o2r", T.kv, 0, 2, "own")
+    s_("o3r", T.kv, 0, 3, "own")
+    twait("lv2", 16)
+    twait("lv3", 16)
+    o_("o2r", T.kv, 0, 2)
+    o_("o3r", T.kv, 0, 3)
+    twait("aq01", nhi)
+    s_("o0p", T.kv, 0, 0, "peer")
+    s_("o1p", T.kv, 0, 1, "peer")
+    twait("aq23", nhi)
+    s_("o2p", T.kv, 0, 2, "peer")
+    s_("o3p", T.kv, 0, 3, "peer")
+    p_(3, 7, [("o3p", T.kv)], None)
+    twait("at01", nof)
+    s_("t0p", T.kvt, 0, 0, "peer")
+    s_("t1p", T.kvt, 0, 1, "peer")
+    p_(0, 6, [("o0p", T.kv), ("t0p", T.kvt)], None)
+    p_(1, 7, [("o1p", T.kv), ("t1p", T.kvt)], "pc3")
+    twait("at2", nof)
+    s_("t2p", T.kvt, 0, 2, "peer")
+    s_("t2r", T.kvt, 0, 2, "own")
+    p_(2, 6, [("o2p", T.kv), ("t2p", T.kvt)], "pc0")
+    o_("t2r", T.kvt, 0, 2)
+    s_("t0r", T.kvt, 0, 0, "own")
+    s_("t1r", T.kvt, 0, 1, "own")
+    o_("t0r", T.kvt, 0, 0)
+    o_("t1r", T.kvt, 0, 1)
+    twait("at3", n1(offa))
+    s_("t3r", T.kvt, 0, 3, "own")
+    twait("ac3", n1(offb))
+    s_("c3r", T.kvc, kc(3), 3, "own")
+    o_("t3r", T.kvt, 0, 3)
+    o_("c3r", T.kvc, kc(3), 3)
+
+    g.wait_ge(S.pc0, 1)
+    g.wait_ge(S.pc1, 1)
+    send([(T.ops[:, 0:256], peer, T.opr[:, 0:256], S.ar01, hi)])
+    g.wait_ge(S.pc2, 1)
+    g.wait_ge(S.pc3, 1)
+    send([(T.ops[:, 256:512], peer, T.opr[:, 256:512], S.ar23, hi)])
+
+    for h in range(4):
+        if h % 2 == 0:
+            g.vector.wait_ge(S["ar01" if h == 0 else "ar23"], nhi)
+        a0 = (2 + h) * 512
+        g.vector.wait_ge(S["ao%d" % h], TOT[h])
+        g.vector.tensor_tensor(T.yo[:, h * P:(h + 1) * P], T.ps[:, a0:a0 + P], T.opr[:, h * P:(h + 1) * P],
+                               AluOpType.add).then_inc(S["fA" if h < 2 else "f%d" % h], 1)
+
+    g.sync.wait_ge(S.fA, 2)
+    g.sync.dma_start(T.y[:, 0:256], T.yo[:, 0:256]).then_inc(S.stA, 16)
+    g.sync.wait_ge(S.f2, 1)
+    g.sync.dma_start(T.y[:, 256:384], T.yo[:, 256:384]).then_inc(S.st2, 16)
+    g.scalar.wait_ge(S.f3, 1)
+    g.scalar.dma_start(T.y[:, 384:512], T.yo[:, 384:512]).then_inc(S.st3, 16)
+    g.sync.wait_ge(S.stA, 16)
+    g.sync.wait_ge(S.st2, 16)
+    g.scalar.wait_ge(S.st3, 16)
     g.wait_ge(S.sent, sent[0])

from concourse.bass import DstId, RemoteDMATransfer
from concourse.mybir import dt, AluOpType, ActivationFunctionType

P = 128
NT = 16
TOT = [2, 2, 2, 3]

SCRATCH = {
    "kv": ("sbuf", [P, 1024], "bfloat16"),
    "qo": ("sbuf", [P, 512], "bfloat16"),
    "kvt": ("sbuf", [P, 1024], "bfloat16"),
    "kvc": ("sbuf", [P, 256], "bfloat16"),
    "qp": ("sbuf", [P, 512], "bfloat16"),
    "sb": ("sbuf", [P, NT * P], "bfloat16"),
    "zero": ("sbuf", [P, P], "float32"),
    "ops": ("sbuf", [P, 512], "bfloat16"),
    "opr": ("sbuf", [P, 512], "bfloat16"),
    "yo": ("sbuf", [P, 512], "bfloat16"),
    "ps": ("psum", [P, 4096], "float32"),
}
SEMAPHORES = (["lk01", "lv01", "lq01", "lk2", "lv2", "lk3", "lv3", "lq23", "z", "sent",
               "at01", "at2", "at3", "ac3", "aq01", "aq23", "ar01", "ar23",
               "fA", "f2", "f3", "stA", "st2", "st3"]
              + [n + str(h) for h in range(4) for n in ("ao", "po", "pc")]
              + [n + str(i) for i in range(NT) for n in ("s", "r")])


def rank_program(g, core, T, topo):
    if T.rank_of(core) is None:
        return
    S = T.sem

    def same_chip(a, b):
        return topo.host(a) == topo.host(b) and topo.chip(a) == topo.chip(b)

    others = [c for c in T.cores if c != core]
    peer = [c for c in others if same_chip(c, core)][0]
    far = [c for c in others if not same_chip(c, core)]
    twin = [c for c in far if topo.die(c) == topo.die(core)][0]
    cross = [c for c in far if c != twin][0]
    off = topo.mask(core, twin)
    hi = topo.mask(core, peer) & ~off
    bits = [1 << b for b in range(off.bit_length()) if off >> b & 1]
    offa, offb = sum(bits[:len(bits) // 2]), sum(bits[len(bits) // 2:])

    def n1(m):
        return bin(m).count("1")

    def kc(h):
        return h * P if h < 2 else 512 + (h - 2) * 256

    def vc(h):
        return 256 + h * P if h < 2 else 640 + (h - 2) * 256

    g.vector.memset(T.zero[:], 0.0).then_inc(S.z, 1)
    g.vector.wait_ge(S.z, 1)
    g.sync.dma_start(T.kv[:, 0:256], T.k[:, 0:256]).then_inc(S.lk01, 16)
    g.scalar.dma_start(T.kv[:, 256:512], T.v[:, 0:256]).then_inc(S.lv01, 16)
    g.sync.dma_start(T.kv[:, kc(2):kc(2) + P], T.k[:, 256:384]).then_inc(S.lk2, 16)
    g.scalar.dma_start(T.kv[:, vc(2):vc(2) + P], T.v[:, 256:384]).then_inc(S.lv2, 16)
    g.sync.dma_start(T.qo[:, 0:256], T.q[:, 0:256]).then_inc(S.lq01, 16)
    g.scalar.dma_start(T.qo[:, 256:512], T.q[:, 256:512]).then_inc(S.lq23, 16)
    g.sync.dma_start(T.kv[:, kc(3):kc(3) + P], T.k[:, 384:512]).then_inc(S.lk3, 16)
    g.scalar.dma_start(T.kv[:, vc(3):vc(3) + P], T.v[:, 384:512]).then_inc(S.lv3, 16)

    sent = [0]

    def send(trs):
        if len(trs) == 1:
            src, d, dst, sem, m = trs[0]
            rid, pid = topo.addr(d, core)
            g.remote_dma(out_ap=dst, in_ap=src, remote_sem=sem, local_sem=S.sent, pid=pid, routing_id=rid,
                         dma_engine_mask=m)
        else:
            lst = []
            for src, d, dst, sem, m in trs:
                rid, pid = topo.addr(d, core)
                lst.append(RemoteDMATransfer(dst_ids=[DstId(rid=rid, pnc=pid)], dma_engine_mask=m, remote_sem=sem,
                                             src=src, dst=dst))
            g.remote_dma_fused(lst, local_sem=S.sent)
        sent[0] += sum(n1(t[4]) for t in trs)

    g.wait_ge(S.lk01, 16)
    g.wait_ge(S.lv01, 16)
    send([(T.kv[:, 0:512], twin, T.kvt[:, 0:512], S.at01, off)])
    g.wait_ge(S.lk2, 16)
    g.wait_ge(S.lv2, 16)
    g.wait_ge(S.lq01, 16)
    send([(T.kv[:, 512:768], twin, T.kvt[:, 512:768], S.at2, off),
          (T.qo[:, 0:256], peer, T.qp[:, 0:256], S.aq01, hi)])
    g.wait_ge(S.lk3, 16)
    g.wait_ge(S.lv3, 16)
    g.wait_ge(S.lq23, 16)
    send([(T.kv[:, 768:1024], twin, T.kvt[:, 768:1024], S.at3, offa),
          (T.kv[:, 768:1024], cross, T.kvc[:, 0:256], S.ac3, offb),
          (T.qo[:, 256:512], peer, T.qp[:, 256:512], S.aq23, hi)])

    nof, nhi = n1(off), n1(hi)
    waited = set()

    def twait(name, val=1):
        if (name, val) not in waited:
            waited.add((name, val))
            g.tensor.wait_ge(S[name], val)

    tile = {}
    done = [0] * 4

    def s_(key, buf, base, h, who):
        i = len(tile)
        tile[key] = i
        if i >= 2:
            twait("r%d" % (i - 2))
        c0 = (i % 2) * 512
        kk = kc(h) - base
        q = T.qo if who == "own" else T.qp
        g.tensor.matmul(T.ps[:, c0:c0 + P], buf[:, kk:kk + P], q[:, h * P:(h + 1) * P],
                        True, True).then_inc(S["s%d" % i], 1)
        if who == "peer":
            g.vector.wait_ge(S["s%d" % i], 1)
            g.vector.tensor_tensor(T.sb[:, i * P:(i + 1) * P], T.ps[:, c0:c0 + P], T.zero[:, 0:P],
                                   AluOpType.max).then_inc(S["r%d" % i], 1)
        else:
            g.scalar.wait_ge(S["s%d" % i], 1)
            g.scalar.activation(T.sb[:, i * P:(i + 1) * P], T.ps[:, c0:c0 + P],
                                ActivationFunctionType.Relu).then_inc(S["r%d" % i], 1)

    def o_(key, buf, base, h):
        i = tile[key]
        twait("r%d" % i)
        vv = vc(h) - base
        a0 = (2 + h) * 512
        g.tensor.matmul(T.ps[:, a0:a0 + P], buf[:, vv:vv + P], T.sb[:, i * P:(i + 1) * P],
                        done[h] == 0, done[h] == TOT[h] - 1).then_inc(S["ao%d" % h], 1)
        done[h] += 1

    def p_(h, bank, parts, free):
        if free:
            twait(free)
        a0 = bank * 512
        for n, (key, buf) in enumerate(parts):
            i = tile[key]
            twait("r%d" % i)
            g.tensor.matmul(T.ps[:, a0:a0 + P], buf[:, vc(h):vc(h) + P], T.sb[:, i * P:(i + 1) * P],
                            n == 0, n == len(parts) - 1).then_inc(S["po%d" % h], 1)
        g.vector.wait_ge(S["po%d" % h], len(parts))
        g.vector.tensor_copy(T.ops[:, h * P:(h + 1) * P], T.ps[:, a0:a0 + P]).then_inc(S["pc%d" % h], 1)

    twait("lk01", 16)
    twait("lq01", 16)
    s_("o0r", T.kv, 0, 0, "own")
    s_("o1r", T.kv, 0, 1, "own")
    twait("lv01", 16)
    o_("o0r", T.kv, 0, 0)
    o_("o1r", T.kv, 0, 1)
    twait("lk2", 16)
    twait("lk3", 16)
    twait("lq23", 16)
    s_("o2r", T.kv, 0, 2, "own")
    s_("o3r", T.kv, 0, 3, "own")
    twait("lv2", 16)
    twait("lv3", 16)
    o_("o2r", T.kv, 0, 2)
    o_("o3r", T.kv, 0, 3)
    twait("aq01", nhi)
    s_("o0p", T.kv, 0, 0, "peer")
    s_("o1p", T.kv, 0, 1, "peer")
    twait("aq23", nhi)
    s_("o2p", T.kv, 0, 2, "peer")
    s_("o3p", T.kv, 0, 3, "peer")
    p_(3, 7, [("o3p", T.kv)], None)
    twait("at01", nof)
    s_("t0p", T.kvt, 0, 0, "peer")
    s_("t1p", T.kvt, 0, 1, "peer")
    p_(0, 6, [("o0p", T.kv), ("t0p", T.kvt)], None)
    p_(1, 7, [("o1p", T.kv), ("t1p", T.kvt)], "pc3")
    twait("at2", nof)
    s_("t2p", T.kvt, 0, 2, "peer")
    s_("t2r", T.kvt, 0, 2, "own")
    p_(2, 6, [("o2p", T.kv), ("t2p", T.kvt)], "pc0")
    o_("t2r", T.kvt, 0, 2)
    s_("t0r", T.kvt, 0, 0, "own")
    s_("t1r", T.kvt, 0, 1, "own")
    o_("t0r", T.kvt, 0, 0)
    o_("t1r", T.kvt, 0, 1)
    twait("at3", n1(offa))
    s_("t3r", T.kvt, 0, 3, "own")
    twait("ac3", n1(offb))
    s_("c3r", T.kvc, kc(3), 3, "own")
    o_("t3r", T.kvt, 0, 3)
    o_("c3r", T.kvc, kc(3), 3)

    g.wait_ge(S.pc0, 1)
    g.wait_ge(S.pc1, 1)
    send([(T.ops[:, 0:256], peer, T.opr[:, 0:256], S.ar01, hi)])
    g.wait_ge(S.pc2, 1)
    g.wait_ge(S.pc3, 1)
    send([(T.ops[:, 256:512], peer, T.opr[:, 256:512], S.ar23, hi)])

    for h in range(4):
        if h % 2 == 0:
            g.vector.wait_ge(S["ar01" if h == 0 else "ar23"], nhi)
        a0 = (2 + h) * 512
        g.vector.wait_ge(S["ao%d" % h], TOT[h])
        g.vector.tensor_tensor(T.yo[:, h * P:(h + 1) * P], T.ps[:, a0:a0 + P], T.opr[:, h * P:(h + 1) * P],
                               AluOpType.add).then_inc(S["fA" if h < 2 else "f%d" % h], 1)

    g.sync.wait_ge(S.fA, 2)
    g.sync.dma_start(T.y[:, 0:256], T.yo[:, 0:256]).then_inc(S.stA, 16)
    g.sync.wait_ge(S.f2, 1)
    g.sync.dma_start(T.y[:, 256:384], T.yo[:, 256:384]).then_inc(S.st2, 16)
    g.scalar.wait_ge(S.f3, 1)
    g.scalar.dma_start(T.y[:, 384:512], T.yo[:, 384:512]).then_inc(S.st3, 16)
    g.sync.wait_ge(S.stA, 16)
    g.sync.wait_ge(S.st2, 16)
    g.scalar.wait_ge(S.st3, 16)
    g.wait_ge(S.sent, sent[0])
